import numpy as np
import ml_dtypes


def mxq(x, axis, fmt="e4m3"):
    dtype, down = {"e4m3": (ml_dtypes.float8_e4m3fn, 7), "e5m2": (ml_dtypes.float8_e5m2, 14)}[fmt]
    v = np.moveaxis(np.asarray(x, np.float32).astype(ml_dtypes.bfloat16).astype(np.float64), axis, -1)
    blocks = v.reshape(v.shape[:-1] + (-1, 32))
    amax = np.abs(blocks).max(-1, keepdims=True)
    byte = np.maximum(np.where(amax > 0, np.frexp(amax)[1] - 1 + 127, 0) - down, 1)
    scale = np.exp2(byte - 127.0)
    codes = (blocks / scale).astype(np.float32).astype(dtype).astype(np.float64)
    return np.moveaxis((codes * scale).reshape(v.shape), -1, axis)


WIDE = False


def mx_kscale(k):
    if not WIDE:
        return np.ones(k)
    levels = np.array([10, -10, 5, -5, 0])
    if k % 512:
        return np.exp2(np.random.permutation(np.resize(levels, k // 32))).repeat(32)
    a = np.empty((k // 512, 16))
    for p in range(k // 512):
        a[p, :8] = np.random.permutation(np.resize(levels, 8))
        for g in range(8):
            far = levels[np.abs(levels - a[p, g]) >= 10]
            a[p, g + 8] = far[np.random.randint(len(far))]
    return np.exp2(a.ravel()).repeat(32)


BF16 = ml_dtypes.bfloat16


def bf(x):
    return np.asarray(x, np.float32).astype(BF16)


def f64(x):
    return np.asarray(x).astype(np.float64)

def planes(Y):
    n, m = Y.shape
    b = f64(bf(Y)).reshape(n // 32, 32, m)
    amax = np.abs(b).max(1)
    byte = np.clip(np.where(amax > 0, np.frexp(amax)[1] - 1 + 127 - 7, 1), 1, 254)
    codes = (b * np.exp2(127.0 - byte)[:, None, :]).reshape(n, m).astype(np.float32).astype(ml_dtypes.float8_e4m3fn).view(np.uint8)
    words = codes.reshape(n // 512, 128, 4, m).transpose(0, 1, 3, 2)
    return np.ascontiguousarray(words), np.ascontiguousarray(byte.astype(np.uint8).reshape(n // 512, 16, m))


B, T, N, C = 4, 512, 1024, 384


def setup_inputs():
    s = mx_kscale(N)
    t = mx_kscale(T)
    rates = np.random.exponential(1.0, (B, T, N)) * s
    recurrent = np.random.randn(N, N) / np.sqrt(N) / s[:, None]
    time_gain = (1.0 + 0.3 * np.random.randn(T)) * t
    readout = 1.5 * np.random.randn(C, T) / np.sqrt(T) / t
    offset = 0.3 * np.random.randn(N)
    neuron_gain = np.exp(0.8 * np.random.randn(N))
    return {"rates": bf(rates), "recurrent": bf(recurrent), "time_gain": bf(time_gain),
            "readout": bf(readout), "offset": bf(offset), "neuron_gain": bf(neuron_gain)}


def reference(rates, recurrent, time_gain, readout, offset, neuron_gain):
    drive = mxq(f64(rates), 2, "e4m3") @ mxq(f64(recurrent), 0, "e4m3")
    activity = np.tanh(drive) * f64(time_gain)[:, None]
    comp = mxq(f64(readout), 1, "e4m3") @ mxq(activity, 1, "e4m3")
    y = (comp + f64(offset)) * f64(neuron_gain)
    Y = y.reshape(B * C, N).T
    words, scales = planes(Y)
    return y, words, scales

@@ -1,0 +1,376 @@
+from contextlib import ExitStack
+
+import concourse.mybir as mybir
+from concourse.masks import make_identity
+
+B, T, N, C = 4, 512, 1024, 384
+FLOPS = 2 * B * T * N * N + 2 * B * C * T * N
+
+F32 = mybir.dt.float32
+BF16 = mybir.dt.bfloat16
+U32 = mybir.dt.uint32
+I32 = mybir.dt.int32
+U8 = mybir.dt.uint8
+FP8X4 = mybir.dt.float8_e4m3fn_x4
+ACT = mybir.ActivationFunctionType
+ALU = mybir.AluOpType
+
+P = 128
+PACK = 4
+KP = P * PACK
+G = N // KP
+CT = C // P
+BANKS = 8
+YG_BUFS = 2
+UNITS = [(0, 0), (1, 0), (0, 1), (1, 1), (2, 0), (2, 1), (3, 0), (3, 1)]
+
+
+def tile_recurrent_rates_temporal_readout_h3_kernel(
+    tc, rates, recurrent, time_gain, readout, offset, neuron_gain, out_0, out_1, out_2
+):
+    nc = tc.nc
+    with ExitStack() as ctx:
+        keep = ctx.enter_context(tc.tile_pool(name="keep", bufs=1))
+        work = ctx.enter_context(tc.tile_pool(name="work", bufs=2))
+        work3 = ctx.enter_context(tc.tile_pool(name="work3", bufs=3))
+        outp = ctx.enter_context(tc.tile_pool(name="outp", bufs=6))
+        psum = ctx.enter_context(tc.psum_pool(name="psum", bufs=1))
+        ctx.enter_context(tc.manual_schedule())
+
+        bank_count = [0]
+
+        def next_bank():
+            k = bank_count[0] % BANKS
+            bank_count[0] = bank_count[0] + 1
+            return psum.tile([P, KP], F32, name="bank%d" % k)
+
+        def copy_on(engine, out, in_):
+            if engine == "scalar":
+                nc.scalar.copy(out=out, in_=in_)
+            else:
+                nc.vector.tensor_copy(out=out, in_=in_)
+
+        def interleave(engine, out, in_):
+            dst = out.rearrange("p (c i) j -> p c j i", i=4)
+            src = in_.rearrange("p j (c i) -> p c j i", i=4)
+            if engine == "gpsimd":
+                nc.gpsimd.tensor_scalar(
+                    out=out, in0=in_.rearrange("p j c -> p c j"), scalar1=1.0, scalar2=0.0, op0=ALU.mult, op1=ALU.add
+                )
+            else:
+                copy_on(engine, dst, src)
+
+        def quantize(codes, scales, grouped):
+            nc.vector.quantize_mx(out=codes.bitcast(FP8X4), scales=scales, in_=grouped)
+
+        r_raw, w_raw = {}, {}
+
+        def load_rates(r, first=0, count=2):
+            b, h = divmod(r, 2)
+            raw = keep.tile([P, count, N], BF16, name="r_raw%d_%d" % (r, first))
+            t0 = 2 * h + first
+            nc.sync.dma_start(out=raw[:], in_=rates[b].rearrange("(p t) k -> p t k", t=PACK)[:, t0 : t0 + count, :])
+            for i in range(count):
+                r_raw[r, first + i] = raw[:, i, :]
+
+        def load_weights(g, n0, width):
+            w_raw[g, n0] = keep.tile([P, PACK, width], BF16, name="w_raw%d_%d" % (g, n0))
+            nc.sync.dma_start(
+                out=w_raw[g, n0][:],
+                in_=recurrent[g * KP : (g + 1) * KP, n0 : n0 + width].rearrange("(p j) n -> p j n", j=PACK),
+            )
+
+        tg = keep.tile([P, PACK], BF16)
+        off_raw = keep.tile([P, G, PACK], BF16)
+        gain_raw = keep.tile([P, G, PACK], BF16)
+        ro_raw = keep.tile([P, CT, T], BF16)
+
+        load_rates(0, 0, 1)
+        load_rates(0, 1, 1)
+        load_weights(0, 0, 256)
+        load_rates(1, 0, 1)
+        load_weights(1, 0, 256)
+        load_rates(1, 1, 1)
+        load_weights(0, 256, 256)
+        load_weights(1, 256, 256)
+        nc.sync.dma_start(out=tg[:], in_=time_gain.rearrange("(p t) -> p t", t=PACK))
+        load_rates(2)
+        load_weights(0, KP, KP)
+        load_rates(3)
+        nc.sync.dma_start(out=ro_raw[:], in_=readout.rearrange("(i c) k -> c i k", c=P))
+        nc.sync.dma_start(out=off_raw[:], in_=offset.rearrange("(g p t) -> p g t", p=P, t=PACK))
+        nc.sync.dma_start(out=gain_raw[:], in_=neuron_gain.rearrange("(g p t) -> p g t", p=P, t=PACK))
+        load_weights(1, KP, KP)
+        for r in range(4, 2 * B):
+            load_rates(r)
+
+        ident = keep.tile([P, P], F32)
+        make_identity(nc, ident[:])
+        warm = keep.tile([P, 1], F32)
+        nc.scalar.activation(out=warm[:], in_=ident[:, 0:1], func=ACT.Tanh)
+
+        r_grp, r_codes, r_scales = {}, {}, {}
+        w_grp, w_codes, w_scales = {}, {}, {}
+        th, act, a_codes, a_scales, y_t, y_grp = {}, {}, {}, {}, {}, {}
+
+        def turn_rates(r, engines):
+            r_grp[r] = work3.tile([P, G, 2, P, PACK], BF16, name="r_grp", align_bytes=64)
+            words = r_grp[r][:].rearrange("p g t r j -> p g t (r j)").bitcast(F32)
+            for t2 in range(2):
+                src = r_raw[r, t2].bitcast(F32)
+                bank = next_bank()
+                view = bank[:].rearrange("p (g u r) -> p g u r", g=G, u=2)
+                for g in range(G):
+                    for u in range(2):
+                        nc.tensor.transpose(view[:, g, u, :], src[:, 256 * g + u : 256 * (g + 1) : 2], ident[:])
+                copy_on(
+                    engines[t2],
+                    words[:, :, t2, :].rearrange("p g (r u) -> p g r u", u=2),
+                    view.rearrange("p g u r -> p g r u"),
+                )
+
+        def quantize_rates(r):
+            r_codes[r] = keep.tile([P, G, 2, P], U32, name="r_codes%d" % r, align_bytes=64)
+            r_scales[r] = keep.tile([P, G, 2, P], U8, name="r_scales%d" % r, align_bytes=64)
+            quantize(
+                r_codes[r][:].rearrange("p g t r -> p (g t r)"),
+                r_scales[r][:].rearrange("p g t r -> p (g t r)"),
+                r_grp[r][:].rearrange("p g t r j -> p (g t r j)"),
+            )
+
+        def group_weights(g, n0, engine):
+            width = w_raw[g, n0].shape[2]
+            w_grp[g, n0] = keep.tile([P, width, PACK], BF16, name="w_grp%d_%d" % (g, n0), align_bytes=64)
+            interleave(engine, w_grp[g, n0][:], w_raw[g, n0][:])
+
+        def quantize_weights(g, n0):
+            width = w_raw[g, n0].shape[2]
+            codes = keep.tile([P, width], U32, name="w_codes%d_%d" % (g, n0), align_bytes=64)
+            scales = keep.tile([P, width], U8, name="w_scales%d_%d" % (g, n0), align_bytes=64)
+            quantize(codes[:], scales[:], w_grp[g, n0][:].rearrange("p n j -> p (n j)"))
+            for c0 in range(0, width, P):
+                w_codes[g, n0 + c0] = codes[:, c0:width]
+                w_scales[g, n0 + c0] = scales[:, c0:width]
+
+        ro_grp = keep.tile([P, C, PACK], BF16, align_bytes=64)
+        ro_codes = keep.tile([P, C], U32, align_bytes=64)
+        ro_scales = keep.tile([P, C], U8, align_bytes=64)
+
+        def turn_readout(engine):
+            words = ro_grp[:].rearrange("p c j -> p (c j)").bitcast(F32).rearrange("p (i r u) -> p i r u", i=CT, u=2)
+            for first, count in ((0, 2), (2, 1)):
+                bank = next_bank()
+                view = bank[:].rearrange("p (i u r) -> p i u r", i=2, u=2)
+                for i in range(count):
+                    src = ro_raw[:, first + i, :].bitcast(F32)
+                    for u in range(2):
+                        nc.tensor.transpose(view[:, i, u, :], src[:, u:256:2], ident[:])
+                copy_on(engine, words[:, first : first + count], view[:, 0:count].rearrange("p i u r -> p i r u"))
+
+        def quantize_384(codes, scales, grouped):
+            flat = grouped.rearrange("p c j -> p (c j)")
+            for c0, c1 in ((0, 256), (256, C)):
+                quantize(codes[:, c0:c1], scales[:, c0:c1], flat[:, PACK * c0 : PACK * c1])
+
+        gain = keep.tile([P, G, PACK], F32)
+        shift = keep.tile([P, G, PACK], F32)
+
+        def prepare_gains():
+            nc.vector.tensor_copy(out=gain[:], in_=gain_raw[:])
+            nc.vector.tensor_tensor(out=shift[:], in0=off_raw[:], in1=gain_raw[:], op=ALU.mult)
+
+        def drive_bank(s, slots, jj, h):
+            b, half = UNITS[s]
+            width = KP // slots
+            run = width // PACK
+            if s not in th:
+                th[s] = work.tile([P, PACK // slots, PACK, P, slots], F32, name="th")
+            bank = next_bank()
+            view = bank[:].rearrange("p (t n) -> p t n", t=slots)
+            n0 = half * KP + jj * width
+            for ts in range(slots):
+                r, t2 = divmod(h * slots + ts, 2)
+                for g in range(G):
+                    nc.tensor.matmul_mx(
+                        out=view[:, ts, :],
+                        lhsT=r_codes[2 * b + r][:, g, t2, :].bitcast(FP8X4),
+                        lhsT_scale=r_scales[2 * b + r][:, g, t2, :],
+                        rhs=w_codes[g, n0][:, 0:width].bitcast(FP8X4),
+                        rhs_scale=w_scales[g, n0][:, 0:width],
+                        start=(g == 0),
+                        stop=(g == G - 1),
+                    )
+            nc.scalar.activation(
+                out=th[s][:, h, :, jj * run : (jj + 1) * run, :],
+                in_=view.rearrange("p t (m j) -> p j m t", j=PACK),
+                func=ACT.Tanh,
+            )
+
+        def scale_activity(s, n0=0, n1=KP):
+            if s not in act:
+                act[s] = work.tile([P, KP, PACK], BF16, name="act", align_bytes=64)
+            nc.vector.tensor_tensor(
+                out=act[s][:, n0:n1, :].rearrange("p n (h t) -> p n h t", t=2),
+                in0=th[s][:].rearrange("p h j m t -> p (j m) h t")[:, n0:n1],
+                in1=tgain.rearrange("p (h t) -> p h t", t=2).unsqueeze(1).to_broadcast([P, n1 - n0, 2, 2]),
+                op=ALU.mult,
+            )
+
+        def scale_quarter(s, jj):
+            if s not in act:
+                act[s] = work.tile([P, KP, PACK], BF16, name="act", align_bytes=64)
+            run = P // PACK
+            ms = slice(jj * run, (jj + 1) * run)
+            nc.vector.tensor_tensor(
+                out=act[s][:].rearrange("p (j m) t -> p j m t", j=PACK)[:, :, ms, :],
+                in0=th[s][:, 0, :, ms, :],
+                in1=tgain.unsqueeze(1).unsqueeze(1).to_broadcast([P, PACK, run, PACK]),
+                op=ALU.mult,
+            )
+
+        def quantize_activity(s):
+            a_codes[s] = work.tile([P, KP], U32, name="a_codes", align_bytes=64)
+            a_scales[s] = work.tile([P, KP], U8, name="a_scales", align_bytes=64)
+            quantize(a_codes[s][:], a_scales[s][:], act[s][:].rearrange("p n j -> p (n j)"))
+
+        def read_out(s, engines):
+            b, half = UNITS[s]
+            y_t[s] = work3.tile([P, PACK, C], F32, name="y_t")
+            for j in range(PACK):
+                bank = next_bank()
+                cols = slice(j * P, (j + 1) * P)
+                for c0, c1 in ((0, 256), (256, C)):
+                    nc.tensor.matmul_mx(
+                        out=bank[:, c0:c1],
+                        lhsT=a_codes[s][:, cols].bitcast(FP8X4),
+                        lhsT_scale=a_scales[s][:, cols],
+                        rhs=ro_codes[:, c0:c1].bitcast(FP8X4),
+                        rhs_scale=ro_scales[:, c0:c1],
+                        start=True,
+                        stop=True,
+                    )
+                if engines[j] == "scalar":
+                    nc.scalar.activation(
+                        out=y_t[s][:, j, :],
+                        in_=bank[:, 0:C],
+                        func=ACT.Identity,
+                        scale=gain[:, half, j : j + 1],
+                        bias=shift[:, half, j : j + 1],
+                    )
+                else:
+                    nc.vector.tensor_scalar(
+                        out=y_t[s][:, j, :],
+                        in0=bank[:, 0:C],
+                        scalar1=gain[:, half, j : j + 1],
+                        scalar2=shift[:, half, j : j + 1],
+                        op0=ALU.mult,
+                        op1=ALU.add,
+                    )
+
+        def group_result(s, engine):
+            y_grp[s] = work.tile([P, C, PACK], BF16, name="y_grp", align_bytes=64, bufs=YG_BUFS)
+            interleave(engine, y_grp[s][:], y_t[s][:])
+
+        early = B - 1
+        y_scales_early = keep.tile([P, G, early * C], U8, align_bytes=64)
+        y_scales_last = keep.tile([P, G, C], U8, align_bytes=64)
+
+        def quantize_result(s):
+            b, half = UNITS[s]
+            y_codes = work3.tile([P, C], U32, name="y_codes", align_bytes=64)
+            if b < early:
+                scales = y_scales_early[:, half, b * C : (b + 1) * C]
+            else:
+                scales = y_scales_last[:, half, :]
+            quantize_384(y_codes[:], scales, y_grp[s][:])
+            nc.sync.dma_start(
+                out=out_1[half, :, b * C : (b + 1) * C, :].rearrange("p m t -> p (m t)").bitcast(I32),
+                in_=y_codes[:].bitcast(I32),
+            )
+
+        def store_scales(tile, m0, m1):
+            for q in range(4):
+                nc.sync.dma_start(
+                    out=out_2[:, 4 * q : 4 * q + 4, m0:m1].rearrange("g r m -> r g m").bitcast(I32),
+                    in_=tile[32 * q : 32 * q + 4, :, :].bitcast(I32),
+                )
+
+        def turn_result(s, engines, queue=nc.sync):
+            b, half = UNITS[s]
+            for i in range(CT):
+                bank = next_bank()
+                view = bank[:].rearrange("c (j p) -> c j p", j=PACK)
+                for j in range(PACK):
+                    nc.tensor.transpose(view[:, j, :], y_t[s][:, j, i * P : (i + 1) * P], ident[:])
+                y = outp.tile([P, KP], F32, name="y")
+                copy_on(engines[i], y[:].rearrange("c (p j) -> c p j", j=PACK), view.rearrange("c j p -> c p j"))
+                queue.dma_start(out=out_0[b, i * P : (i + 1) * P, half * KP : (half + 1) * KP], in_=y[:])
+
+        tgain = tg[:]
+        S, V = "scalar", "vector"
+        n_units = len(UNITS)
+        last = n_units - 1
+
+        turn_rates(0, [S, S])
+        group_weights(0, 0, V)
+        group_weights(1, 0, V)
+        turn_rates(1, [S, S])
+        quantize_weights(0, 0)
+        quantize_rates(0)
+        quantize_weights(1, 0)
+        drive_bank(0, 2, 0, 0)
+        group_weights(0, 256, V)
+        quantize_rates(1)
+        group_weights(1, 256, V)
+        quantize_weights(0, 256)
+        quantize_weights(1, 256)
+        drive_bank(0, 2, 0, 1)
+        turn_rates(2, [S, S])
+        group_weights(0, KP, V)
+        quantize_rates(2)
+        quantize_weights(0, KP)
+        drive_bank(0, 2, 1, 0)
+        drive_bank(0, 2, 1, 1)
+        turn_rates(3, [S, S])
+        scale_activity(0, 0, 256)
+        quantize_rates(3)
+        scale_activity(0, 256, KP)
+        prepare_gains()
+
+        for s in range(1, last):
+            for h in range(2):
+                for jj in range(2):
+                    drive_bank(s, 2, jj, h)
+                if s == 1 and h == 0:
+                    turn_readout(S)
+                    quantize_activity(0)
+                    quantize_384(ro_codes[:], ro_scales[:], ro_grp[:])
+                    group_weights(1, KP, V)
+            if s == 1:
+                quantize_weights(1, KP)
+            scale_activity(s)
+            read_out(s - 1, [S] * 4)
+            group_result(s - 1, V)
+            quantize_activity(s)
+            if s >= 2:
+                turn_result(s - 2, [S, S, V] if s == 5 else [S] * 3)
+            if s <= 4:
+                turn_rates(s + 3, [S, S] if s <= 1 else [V, V])
+            quantize_result(s - 1)
+            if s <= 4:
+                quantize_rates(s + 3)
+        store_scales(y_scales_early, 0, early * C)
+        for jj in range(PACK):
+            drive_bank(last, PACK, jj, 0)
+            scale_quarter(last, jj)
+        quantize_activity(last)
+        read_out(last - 1, [S] * 4)
+        turn_result(last - 2, [S, S, V])
+        read_out(last, [V, V, S, S])
+        group_result(last - 1, V)
+        turn_result(last - 1, [S, S, S])
+        group_result(last, V)
+        quantize_result(last - 1)
+        quantize_result(last)
+        turn_result(last, [S, S, V])
+        store_scales(y_scales_last, early * C, B * C)

@@ -12,17 +12,23 @@ U32 = mybir.dt.uint32
 I32 = mybir.dt.int32
 U8 = mybir.dt.uint8
 FP8X4 = mybir.dt.float8_e4m3fn_x4
-ACT = mybir.ActivationFunctionType
+FUNC = mybir.ActivationFunctionType
 ALU = mybir.AluOpType
+SCALAR, VECTOR, GPSIMD = "scalar", "vector", "gpsimd"
 
 P = 128
 PACK = 4
-KP = P * PACK
-G = N // KP
-CT = C // P
-BANKS = 8
-YG_BUFS = 2
+K_PASS = P * PACK
+PASS_WORDS = K_PASS // 2
+PASSES = N // K_PASS
+C_TILES = C // P
+CHUNK = 256
+RUN = CHUNK // PACK
+C_PARTS = ((0, 256), (256, C))
+TURNING_BANKS = 7
+
 UNITS = [(0, 0), (1, 0), (0, 1), (1, 1), (2, 0), (2, 1), (3, 0), (3, 1)]
+LAST = len(UNITS) - 1
 
 
 def tile_recurrent_rates_temporal_readout_h3_kernel(
@@ -31,98 +37,100 @@ def tile_recurrent_rates_temporal_readout_h3_kernel(
     nc = tc.nc
     with ExitStack() as ctx:
         keep = ctx.enter_context(tc.tile_pool(name="keep", bufs=1))
-        work = ctx.enter_context(tc.tile_pool(name="work", bufs=2))
+        work2 = ctx.enter_context(tc.tile_pool(name="work2", bufs=2))
         work3 = ctx.enter_context(tc.tile_pool(name="work3", bufs=3))
-        outp = ctx.enter_context(tc.tile_pool(name="outp", bufs=6))
+        outp = ctx.enter_context(tc.tile_pool(name="outp", bufs=2 * C_TILES))
         psum = ctx.enter_context(tc.psum_pool(name="psum", bufs=1))
         ctx.enter_context(tc.manual_schedule())
 
-        bank_count = [0]
+        banks_taken = [0]
 
         def next_bank():
-            k = bank_count[0] % BANKS
-            bank_count[0] = bank_count[0] + 1
-            return psum.tile([P, KP], F32, name="bank%d" % k)
+            k = banks_taken[0] % TURNING_BANKS
+            banks_taken[0] = banks_taken[0] + 1
+            return psum.tile([P, K_PASS], F32, name="bank%d" % k)
 
         def copy_on(engine, out, in_):
-            if engine == "scalar":
+            if engine == SCALAR:
                 nc.scalar.copy(out=out, in_=in_)
             else:
                 nc.vector.tensor_copy(out=out, in_=in_)
 
         def interleave(engine, out, in_):
-            dst = out.rearrange("p (c i) j -> p c j i", i=4)
-            src = in_.rearrange("p j (c i) -> p c j i", i=4)
-            if engine == "gpsimd":
+            if engine == GPSIMD:
                 nc.gpsimd.tensor_scalar(
                     out=out, in0=in_.rearrange("p j c -> p c j"), scalar1=1.0, scalar2=0.0, op0=ALU.mult, op1=ALU.add
                 )
             else:
-                copy_on(engine, dst, src)
+                copy_on(engine, out.rearrange("p (c i) j -> p c j i", i=4), in_.rearrange("p j (c i) -> p c j i", i=4))
 
         def quantize(codes, scales, grouped):
             nc.vector.quantize_mx(out=codes.bitcast(FP8X4), scales=scales, in_=grouped)
 
-        r_raw, w_raw = {}, {}
+        def quantize_components(codes, scales, grouped):
+            flat = grouped.rearrange("p c j -> p (c j)")
+            for c0, c1 in C_PARTS:
+                quantize(codes[:, c0:c1], scales[:, c0:c1], flat[:, PACK * c0 : PACK * c1])
+
+        rates_raw, weights_raw = {}, {}
 
         def load_rates(r, first=0, count=2):
             b, h = divmod(r, 2)
-            raw = keep.tile([P, count, N], BF16, name="r_raw%d_%d" % (r, first))
+            raw = keep.tile([P, count, N], BF16, name="rates_raw%d_%d" % (r, first))
             t0 = 2 * h + first
             nc.sync.dma_start(out=raw[:], in_=rates[b].rearrange("(p t) k -> p t k", t=PACK)[:, t0 : t0 + count, :])
             for i in range(count):
-                r_raw[r, first + i] = raw[:, i, :]
+                rates_raw[r, first + i] = raw[:, i, :]
 
         def load_weights(g, n0, width):
-            w_raw[g, n0] = keep.tile([P, PACK, width], BF16, name="w_raw%d_%d" % (g, n0))
-            nc.sync.dma_start(
-                out=w_raw[g, n0][:],
-                in_=recurrent[g * KP : (g + 1) * KP, n0 : n0 + width].rearrange("(p j) n -> p j n", j=PACK),
-            )
+            weights_raw[g, n0] = keep.tile([P, PACK, width], BF16, name="weights_raw%d_%d" % (g, n0))
+            rows = recurrent[g * K_PASS : (g + 1) * K_PASS, n0 : n0 + width]
+            nc.sync.dma_start(out=weights_raw[g, n0][:], in_=rows.rearrange("(p j) n -> p j n", j=PACK))
 
-        tg = keep.tile([P, PACK], BF16)
-        off_raw = keep.tile([P, G, PACK], BF16)
-        gain_raw = keep.tile([P, G, PACK], BF16)
-        ro_raw = keep.tile([P, CT, T], BF16)
+        time_raw = keep.tile([P, PACK], BF16)
+        offset_raw = keep.tile([P, PASSES, PACK], BF16)
+        gain_raw = keep.tile([P, PASSES, PACK], BF16)
+        readout_raw = keep.tile([P, C_TILES, T], BF16)
 
+        nc.scalar.dma_start(out=time_raw[:], in_=time_gain.rearrange("(p t) -> p t", t=PACK))
         load_rates(0, 0, 1)
         load_rates(0, 1, 1)
-        load_weights(0, 0, 256)
+        load_weights(0, 0, CHUNK)
         load_rates(1, 0, 1)
-        load_weights(1, 0, 256)
+        load_weights(1, 0, CHUNK)
         load_rates(1, 1, 1)
-        load_weights(0, 256, 256)
-        load_weights(1, 256, 256)
-        nc.sync.dma_start(out=tg[:], in_=time_gain.rearrange("(p t) -> p t", t=PACK))
+        load_weights(0, CHUNK, CHUNK)
+        load_weights(1, CHUNK, CHUNK)
         load_rates(2)
-        load_weights(0, KP, KP)
+        load_weights(0, K_PASS, K_PASS)
         load_rates(3)
-        nc.sync.dma_start(out=ro_raw[:], in_=readout.rearrange("(i c) k -> c i k", c=P))
-        nc.sync.dma_start(out=off_raw[:], in_=offset.rearrange("(g p t) -> p g t", p=P, t=PACK))
+        load_weights(1, K_PASS, K_PASS)
+        nc.sync.dma_start(out=readout_raw[:], in_=readout.rearrange("(i c) k -> c i k", c=P))
+        nc.sync.dma_start(out=offset_raw[:], in_=offset.rearrange("(g p t) -> p g t", p=P, t=PACK))
         nc.sync.dma_start(out=gain_raw[:], in_=neuron_gain.rearrange("(g p t) -> p g t", p=P, t=PACK))
-        load_weights(1, KP, KP)
         for r in range(4, 2 * B):
             load_rates(r)
 
         ident = keep.tile([P, P], F32)
         make_identity(nc, ident[:])
-        warm = keep.tile([P, 1], F32)
-        nc.scalar.activation(out=warm[:], in_=ident[:, 0:1], func=ACT.Tanh)
+        table_warm_up = keep.tile([P, 1], F32)
+        nc.scalar.activation(out=table_warm_up[:], in_=ident[:, 0:1], func=FUNC.Tanh)
 
-        r_grp, r_codes, r_scales = {}, {}, {}
-        w_grp, w_codes, w_scales = {}, {}, {}
-        th, act, a_codes, a_scales, y_t, y_grp = {}, {}, {}, {}, {}, {}
+        rates_grouped, rates_codes, rates_scales = {}, {}, {}
+        weights_grouped, weights_codes, weights_scales = {}, {}, {}
+        tanh_drive, activity, activity_codes, activity_scales, y_neurons, y_grouped = {}, {}, {}, {}, {}, {}
 
         def turn_rates(r, engines):
-            r_grp[r] = work3.tile([P, G, 2, P, PACK], BF16, name="r_grp", align_bytes=64)
-            words = r_grp[r][:].rearrange("p g t r j -> p g t (r j)").bitcast(F32)
+            rates_grouped[r] = work3.tile([P, PASSES, 2, P, PACK], BF16, name="rates_grouped", align_bytes=64)
+            words = rates_grouped[r][:].rearrange("p g t r j -> p g t (r j)").bitcast(F32)
             for t2 in range(2):
-                src = r_raw[r, t2].bitcast(F32)
+                src = rates_raw[r, t2].bitcast(F32)
                 bank = next_bank()
-                view = bank[:].rearrange("p (g u r) -> p g u r", g=G, u=2)
-                for g in range(G):
+                view = bank[:].rearrange("p (g u r) -> p g u r", g=PASSES, u=2)
+                for g in range(PASSES):
                     for u in range(2):
-                        nc.tensor.transpose(view[:, g, u, :], src[:, 256 * g + u : 256 * (g + 1) : 2], ident[:])
+                        every_second = src[:, PASS_WORDS * g + u : PASS_WORDS * (g + 1) : 2]
+                        nc.tensor.transpose(view[:, g, u, :], every_second, ident[:])
                 copy_on(
                     engines[t2],
                     words[:, :, t2, :].rearrange("p g (r u) -> p g r u", u=2),
@@ -130,247 +138,249 @@ def tile_recurrent_rates_temporal_readout_h3_kernel(
                 )
 
         def quantize_rates(r):
-            r_codes[r] = keep.tile([P, G, 2, P], U32, name="r_codes%d" % r, align_bytes=64)
-            r_scales[r] = keep.tile([P, G, 2, P], U8, name="r_scales%d" % r, align_bytes=64)
+            rates_codes[r] = keep.tile([P, PASSES, 2, P], U32, name="rates_codes%d" % r, align_bytes=64)
+            rates_scales[r] = keep.tile([P, PASSES, 2, P], U8, name="rates_scales%d" % r, align_bytes=64)
             quantize(
-                r_codes[r][:].rearrange("p g t r -> p (g t r)"),
-                r_scales[r][:].rearrange("p g t r -> p (g t r)"),
-                r_grp[r][:].rearrange("p g t r j -> p (g t r j)"),
+                rates_codes[r][:].rearrange("p g t r -> p (g t r)"),
+                rates_scales[r][:].rearrange("p g t r -> p (g t r)"),
+                rates_grouped[r][:].rearrange("p g t r j -> p (g t r j)"),
             )
 
         def group_weights(g, n0, engine):
-            width = w_raw[g, n0].shape[2]
-            w_grp[g, n0] = keep.tile([P, width, PACK], BF16, name="w_grp%d_%d" % (g, n0), align_bytes=64)
-            interleave(engine, w_grp[g, n0][:], w_raw[g, n0][:])
+            width = weights_raw[g, n0].shape[2]
+            name = "shared_grouped" if width == K_PASS else "weights_grouped%d_%d" % (g, n0)
+            weights_grouped[g, n0] = keep.tile([P, width, PACK], BF16, name=name, align_bytes=64)
+            interleave(engine, weights_grouped[g, n0][:], weights_raw[g, n0][:])
 
         def quantize_weights(g, n0):
-            width = w_raw[g, n0].shape[2]
-            codes = keep.tile([P, width], U32, name="w_codes%d_%d" % (g, n0), align_bytes=64)
-            scales = keep.tile([P, width], U8, name="w_scales%d_%d" % (g, n0), align_bytes=64)
-            quantize(codes[:], scales[:], w_grp[g, n0][:].rearrange("p n j -> p (n j)"))
-            for c0 in range(0, width, P):
-                w_codes[g, n0 + c0] = codes[:, c0:width]
-                w_scales[g, n0 + c0] = scales[:, c0:width]
+            width = weights_raw[g, n0].shape[2]
+            codes = keep.tile([P, width], U32, name="weights_codes%d_%d" % (g, n0), align_bytes=64)
+            scales = keep.tile([P, width], U8, name="weights_scales%d_%d" % (g, n0), align_bytes=64)
+            quantize(codes[:], scales[:], weights_grouped[g, n0][:].rearrange("p n j -> p (n j)"))
+            for c0 in range(0, width, CHUNK):
+                weights_codes[g, n0 + c0] = codes[:, c0 : c0 + CHUNK]
+                weights_scales[g, n0 + c0] = scales[:, c0 : c0 + CHUNK]
 
-        ro_grp = keep.tile([P, C, PACK], BF16, align_bytes=64)
-        ro_codes = keep.tile([P, C], U32, align_bytes=64)
-        ro_scales = keep.tile([P, C], U8, align_bytes=64)
+        readout_grouped = keep.tile([P, C, PACK], BF16, align_bytes=64)
+        readout_codes = keep.tile([P, C], U32, align_bytes=64)
+        readout_scales = keep.tile([P, C], U8, align_bytes=64)
 
-        def turn_readout(engine):
-            words = ro_grp[:].rearrange("p c j -> p (c j)").bitcast(F32).rearrange("p (i r u) -> p i r u", i=CT, u=2)
-            for first, count in ((0, 2), (2, 1)):
+        def turn_readout():
+            words = readout_grouped[:].rearrange("p c j -> p (c j)").bitcast(F32)
+            words = words.rearrange("p (i r u) -> p i r u", i=C_TILES, u=2)
+            for first in range(0, C_TILES, 2):
+                count = min(2, C_TILES - first)
                 bank = next_bank()
                 view = bank[:].rearrange("p (i u r) -> p i u r", i=2, u=2)
                 for i in range(count):
-                    src = ro_raw[:, first + i, :].bitcast(F32)
+                    src = readout_raw[:, first + i, :].bitcast(F32)
                     for u in range(2):
-                        nc.tensor.transpose(view[:, i, u, :], src[:, u:256:2], ident[:])
-                copy_on(engine, words[:, first : first + count], view[:, 0:count].rearrange("p i u r -> p i r u"))
+                        nc.tensor.transpose(view[:, i, u, :], src[:, u:PASS_WORDS:2], ident[:])
+                nc.scalar.copy(out=words[:, first : first + count], in_=view[:, 0:count].rearrange("p i u r -> p i r u"))
 
-        def quantize_384(codes, scales, grouped):
-            flat = grouped.rearrange("p c j -> p (c j)")
-            for c0, c1 in ((0, 256), (256, C)):
-                quantize(codes[:, c0:c1], scales[:, c0:c1], flat[:, PACK * c0 : PACK * c1])
+        gain = keep.tile([P, PASSES, PACK], F32)
+        shift = keep.tile([P, PASSES, PACK], F32)
 
-        gain = keep.tile([P, G, PACK], F32)
-        shift = keep.tile([P, G, PACK], F32)
-
-        def prepare_gains():
+        def prepare_gain_and_shift():
             nc.vector.tensor_copy(out=gain[:], in_=gain_raw[:])
-            nc.vector.tensor_tensor(out=shift[:], in0=off_raw[:], in1=gain_raw[:], op=ALU.mult)
+            nc.vector.tensor_tensor(out=shift[:], in0=offset_raw[:], in1=gain_raw[:], op=ALU.mult)
 
-        def drive_bank(s, slots, jj, h):
-            b, half = UNITS[s]
-            width = KP // slots
-            run = width // PACK
-            if s not in th:
-                th[s] = work.tile([P, PACK // slots, PACK, P, slots], F32, name="th")
+        time_columns = keep.tile([P, P], F32)
+        time_rows = keep.tile([P, P], F32)
+        time_bank = psum.tile([P, K_PASS], F32, name="time_bank")
+
+        def time_gain_to_rows():
+            nc.gpsimd.memset(time_columns[:], 0.0)
+            nc.gpsimd.tensor_copy(out=time_columns[:, 0:PACK], in_=time_raw[:])
             bank = next_bank()
-            view = bank[:].rearrange("p (t n) -> p t n", t=slots)
-            n0 = half * KP + jj * width
-            for ts in range(slots):
-                r, t2 = divmod(h * slots + ts, 2)
-                for g in range(G):
+            nc.tensor.transpose(bank[:, 0:P], time_columns[:], ident[:])
+            nc.scalar.copy(out=time_rows[:], in_=bank[:, 0:P])
+
+        def time_gain_to_psum():
+            nc.tensor.transpose(time_bank[:, 0:P], time_rows[:], ident[:])
+
+        def drive_bank(s, q, h):
+            b, half = UNITS[s]
+            if s not in tanh_drive:
+                tanh_drive[s] = work2.tile([P, 2, 2, PACK, RUN, 2], F32, name="tanh_drive")
+            bank = next_bank()
+            view = bank[:].rearrange("p (t n) -> p t n", t=2)
+            n0 = half * K_PASS + q * CHUNK
+            for t2 in range(2):
+                for g in range(PASSES):
                     nc.tensor.matmul_mx(
-                        out=view[:, ts, :],
-                        lhsT=r_codes[2 * b + r][:, g, t2, :].bitcast(FP8X4),
-                        lhsT_scale=r_scales[2 * b + r][:, g, t2, :],
-                        rhs=w_codes[g, n0][:, 0:width].bitcast(FP8X4),
-                        rhs_scale=w_scales[g, n0][:, 0:width],
+                        out=view[:, t2, :],
+                        lhsT=rates_codes[2 * b + h][:, g, t2, :].bitcast(FP8X4),
+                        lhsT_scale=rates_scales[2 * b + h][:, g, t2, :],
+                        rhs=weights_codes[g, n0].bitcast(FP8X4),
+                        rhs_scale=weights_scales[g, n0],
                         start=(g == 0),
-                        stop=(g == G - 1),
+                        stop=(g == PASSES - 1),
                     )
             nc.scalar.activation(
-                out=th[s][:, h, :, jj * run : (jj + 1) * run, :],
-                in_=view.rearrange("p t (m j) -> p j m t", j=PACK),
-                func=ACT.Tanh,
+                out=tanh_drive[s][:, h, q], in_=view.rearrange("p t (m j) -> p j m t", j=PACK), func=FUNC.Tanh
             )
 
-        def scale_activity(s, n0=0, n1=KP):
-            if s not in act:
-                act[s] = work.tile([P, KP, PACK], BF16, name="act", align_bytes=64)
+        def scale_activity(s, q):
+            if s not in activity:
+                activity[s] = work2.tile([P, K_PASS, PACK], BF16, name="activity", align_bytes=64)
+            factor = time_bank[:, 0:PACK].rearrange("p (h t) -> p h t", t=2).unsqueeze(1).unsqueeze(1)
             nc.vector.tensor_tensor(
-                out=act[s][:, n0:n1, :].rearrange("p n (h t) -> p n h t", t=2),
-                in0=th[s][:].rearrange("p h j m t -> p (j m) h t")[:, n0:n1],
-                in1=tgain.rearrange("p (h t) -> p h t", t=2).unsqueeze(1).to_broadcast([P, n1 - n0, 2, 2]),
-                op=ALU.mult,
-            )
-
-        def scale_quarter(s, jj):
-            if s not in act:
-                act[s] = work.tile([P, KP, PACK], BF16, name="act", align_bytes=64)
-            run = P // PACK
-            ms = slice(jj * run, (jj + 1) * run)
-            nc.vector.tensor_tensor(
-                out=act[s][:].rearrange("p (j m) t -> p j m t", j=PACK)[:, :, ms, :],
-                in0=th[s][:, 0, :, ms, :],
-                in1=tgain.unsqueeze(1).unsqueeze(1).to_broadcast([P, PACK, run, PACK]),
+                out=activity[s][:].rearrange("p (j q m) (h t) -> p q j m h t", j=PACK, q=2, h=2)[:, q],
+                in0=tanh_drive[s][:, :, q].rearrange("p h j m t -> p j m h t"),
+                in1=factor.to_broadcast([P, PACK, RUN, 2, 2]),
                 op=ALU.mult,
             )
 
         def quantize_activity(s):
-            a_codes[s] = work.tile([P, KP], U32, name="a_codes", align_bytes=64)
-            a_scales[s] = work.tile([P, KP], U8, name="a_scales", align_bytes=64)
-            quantize(a_codes[s][:], a_scales[s][:], act[s][:].rearrange("p n j -> p (n j)"))
+            activity_codes[s] = work2.tile([P, K_PASS], U32, name="activity_codes", align_bytes=64)
+            activity_scales[s] = work2.tile([P, K_PASS], U8, name="activity_scales", align_bytes=64)
+            quantize(activity_codes[s][:], activity_scales[s][:], activity[s][:].rearrange("p n j -> p (n j)"))
 
         def read_out(s, engines):
-            b, half = UNITS[s]
-            y_t[s] = work3.tile([P, PACK, C], F32, name="y_t")
+            half = UNITS[s][1]
+            y_neurons[s] = work3.tile([P, PACK, C], F32, name="y_neurons")
             for j in range(PACK):
                 bank = next_bank()
                 cols = slice(j * P, (j + 1) * P)
-                for c0, c1 in ((0, 256), (256, C)):
+                for c0, c1 in C_PARTS:
                     nc.tensor.matmul_mx(
                         out=bank[:, c0:c1],
-                        lhsT=a_codes[s][:, cols].bitcast(FP8X4),
-                        lhsT_scale=a_scales[s][:, cols],
-                        rhs=ro_codes[:, c0:c1].bitcast(FP8X4),
-                        rhs_scale=ro_scales[:, c0:c1],
+                        lhsT=activity_codes[s][:, cols].bitcast(FP8X4),
+                        lhsT_scale=activity_scales[s][:, cols],
+                        rhs=readout_codes[:, c0:c1].bitcast(FP8X4),
+                        rhs_scale=readout_scales[:, c0:c1],
                         start=True,
                         stop=True,
                     )
-                if engines[j] == "scalar":
+                factor, addend = gain[:, half, j : j + 1], shift[:, half, j : j + 1]
+                if engines[j] == SCALAR:
                     nc.scalar.activation(
-                        out=y_t[s][:, j, :],
-                        in_=bank[:, 0:C],
-                        func=ACT.Identity,
-                        scale=gain[:, half, j : j + 1],
-                        bias=shift[:, half, j : j + 1],
+                        out=y_neurons[s][:, j, :], in_=bank[:, 0:C], func=FUNC.Identity, scale=factor, bias=addend
                     )
                 else:
                     nc.vector.tensor_scalar(
-                        out=y_t[s][:, j, :],
+                        out=y_neurons[s][:, j, :],
                         in0=bank[:, 0:C],
-                        scalar1=gain[:, half, j : j + 1],
-                        scalar2=shift[:, half, j : j + 1],
+                        scalar1=factor,
+                        scalar2=addend,
                         op0=ALU.mult,
                         op1=ALU.add,
                     )
 
-        def group_result(s, engine):
-            y_grp[s] = work.tile([P, C, PACK], BF16, name="y_grp", align_bytes=64, bufs=YG_BUFS)
-            interleave(engine, y_grp[s][:], y_t[s][:])
+        def turn_result(s, engines):
+            b, half = UNITS[s]
+            for i in range(C_TILES):
+                bank = next_bank()
+                view = bank[:].rearrange("c (j p) -> c j p", j=PACK)
+                for j in range(PACK):
+                    nc.tensor.transpose(view[:, j, :], y_neurons[s][:, j, i * P : (i + 1) * P], ident[:])
+                y = outp.tile([P, K_PASS], F32, name="y")
+                copy_on(engines[i], y[:].rearrange("c (p j) -> c p j", j=PACK), view.rearrange("c j p -> c p j"))
+                nc.sync.dma_start(out=out_0[b, i * P : (i + 1) * P, half * K_PASS : (half + 1) * K_PASS], in_=y[:])
 
-        early = B - 1
-        y_scales_early = keep.tile([P, G, early * C], U8, align_bytes=64)
-        y_scales_last = keep.tile([P, G, C], U8, align_bytes=64)
+        def group_result(s, engine):
+            if engine == GPSIMD:
+                y_grouped[s] = keep.tile([P, C, PACK], BF16, name="shared_grouped", align_bytes=64)
+            else:
+                y_grouped[s] = keep.tile([P, C, PACK], BF16, name="y_grouped", align_bytes=64)
+            interleave(engine, y_grouped[s][:], y_neurons[s][:])
+
+        early_columns = (B - 1) * C
+        y_scales_early = keep.tile([P, PASSES, early_columns], U8, align_bytes=64)
+        y_scales_last = keep.tile([P, PASSES, C], U8, align_bytes=64)
 
         def quantize_result(s):
             b, half = UNITS[s]
             y_codes = work3.tile([P, C], U32, name="y_codes", align_bytes=64)
-            if b < early:
+            if b < B - 1:
                 scales = y_scales_early[:, half, b * C : (b + 1) * C]
             else:
                 scales = y_scales_last[:, half, :]
-            quantize_384(y_codes[:], scales, y_grp[s][:])
+            quantize_components(y_codes[:], scales, y_grouped[s][:])
             nc.sync.dma_start(
                 out=out_1[half, :, b * C : (b + 1) * C, :].rearrange("p m t -> p (m t)").bitcast(I32),
                 in_=y_codes[:].bitcast(I32),
             )
 
         def store_scales(tile, m0, m1):
-            for q in range(4):
+            for quadrant in range(4):
                 nc.sync.dma_start(
-                    out=out_2[:, 4 * q : 4 * q + 4, m0:m1].rearrange("g r m -> r g m").bitcast(I32),
-                    in_=tile[32 * q : 32 * q + 4, :, :].bitcast(I32),
+                    out=out_2[:, 4 * quadrant : 4 * quadrant + 4, m0:m1].rearrange("g r m -> r g m").bitcast(I32),
+                    in_=tile[32 * quadrant : 32 * quadrant + 4, :, :].bitcast(I32),
                 )
 
-        def turn_result(s, engines, queue=nc.sync):
-            b, half = UNITS[s]
-            for i in range(CT):
-                bank = next_bank()
-                view = bank[:].rearrange("c (j p) -> c j p", j=PACK)
-                for j in range(PACK):
-                    nc.tensor.transpose(view[:, j, :], y_t[s][:, j, i * P : (i + 1) * P], ident[:])
-                y = outp.tile([P, KP], F32, name="y")
-                copy_on(engines[i], y[:].rearrange("c (p j) -> c p j", j=PACK), view.rearrange("c j p -> c p j"))
-                queue.dma_start(out=out_0[b, i * P : (i + 1) * P, half * KP : (half + 1) * KP], in_=y[:])
-
-        tgain = tg[:]
-        S, V = "scalar", "vector"
-        n_units = len(UNITS)
-        last = n_units - 1
-
-        turn_rates(0, [S, S])
-        group_weights(0, 0, V)
-        group_weights(1, 0, V)
-        turn_rates(1, [S, S])
-        quantize_weights(0, 0)
+        turn_rates(0, [VECTOR, SCALAR])
+        time_gain_to_rows()
+        group_weights(0, 0, VECTOR)
+        turn_rates(1, [SCALAR, SCALAR])
+        group_weights(1, 0, VECTOR)
+        group_weights(0, CHUNK, SCALAR)
+        time_gain_to_psum()
         quantize_rates(0)
+        quantize_weights(0, 0)
         quantize_weights(1, 0)
-        drive_bank(0, 2, 0, 0)
-        group_weights(0, 256, V)
+        group_weights(1, CHUNK, VECTOR)
+        drive_bank(0, 0, 0)
         quantize_rates(1)
-        group_weights(1, 256, V)
-        quantize_weights(0, 256)
-        quantize_weights(1, 256)
-        drive_bank(0, 2, 0, 1)
-        turn_rates(2, [S, S])
-        group_weights(0, KP, V)
+        drive_bank(0, 0, 1)
+        quantize_weights(0, CHUNK)
+        quantize_weights(1, CHUNK)
+        turn_rates(2, [SCALAR, SCALAR])
+        group_weights(0, K_PASS, VECTOR)
+        drive_bank(0, 1, 0)
+        drive_bank(0, 1, 1)
+        scale_activity(0, 0)
         quantize_rates(2)
-        quantize_weights(0, KP)
-        drive_bank(0, 2, 1, 0)
-        drive_bank(0, 2, 1, 1)
-        turn_rates(3, [S, S])
-        scale_activity(0, 0, 256)
+        quantize_weights(0, K_PASS)
+        turn_rates(3, [SCALAR, SCALAR])
+        scale_activity(0, 1)
         quantize_rates(3)
-        scale_activity(0, 256, KP)
-        prepare_gains()
+        prepare_gain_and_shift()
 
-        for s in range(1, last):
-            for h in range(2):
-                for jj in range(2):
-                    drive_bank(s, 2, jj, h)
-                if s == 1 and h == 0:
-                    turn_readout(S)
-                    quantize_activity(0)
-                    quantize_384(ro_codes[:], ro_scales[:], ro_grp[:])
-                    group_weights(1, KP, V)
-            if s == 1:
-                quantize_weights(1, KP)
-            scale_activity(s)
-            read_out(s - 1, [S] * 4)
-            group_result(s - 1, V)
-            quantize_activity(s)
-            if s >= 2:
-                turn_result(s - 2, [S, S, V] if s == 5 else [S] * 3)
-            if s <= 4:
-                turn_rates(s + 3, [S, S] if s <= 1 else [V, V])
-            quantize_result(s - 1)
-            if s <= 4:
-                quantize_rates(s + 3)
-        store_scales(y_scales_early, 0, early * C)
-        for jj in range(PACK):
-            drive_bank(last, PACK, jj, 0)
-            scale_quarter(last, jj)
-        quantize_activity(last)
-        read_out(last - 1, [S] * 4)
-        turn_result(last - 2, [S, S, V])
-        read_out(last, [V, V, S, S])
-        group_result(last - 1, V)
-        turn_result(last - 1, [S, S, S])
-        group_result(last, V)
-        quantize_result(last - 1)
-        quantize_result(last)
-        turn_result(last, [S, S, V])
-        store_scales(y_scales_last, early * C, B * C)
+        drive_bank(1, 0, 0)
+        drive_bank(1, 1, 0)
+        turn_readout()
+        quantize_activity(0)
+        quantize_components(readout_codes[:], readout_scales[:], readout_grouped[:])
+        group_weights(1, K_PASS, VECTOR)
+        drive_bank(1, 0, 1)
+        drive_bank(1, 1, 1)
+        quantize_weights(1, K_PASS)
+        scale_activity(1, 0)
+        scale_activity(1, 1)
+        read_out(0, [SCALAR] * PACK)
+        turn_rates(4, [SCALAR, SCALAR])
+
+        for s in range(2, LAST + 1):
+            pair = s + 2
+            if 4 < pair < 2 * B:
+                turn_rates(pair, [VECTOR, VECTOR])
+            drive_bank(s, 0, 0)
+            drive_bank(s, 0, 1)
+            quantize_activity(s - 1)
+            drive_bank(s, 1, 0)
+            drive_bank(s, 1, 1)
+            if pair < 2 * B:
+                quantize_rates(pair)
+            if s >= 3:
+                quantize_result(s - 3)
+            group_result(s - 2, GPSIMD)
+            scale_activity(s, 0)
+            scale_activity(s, 1)
+            turn_result(s - 2, [SCALAR] * C_TILES)
+            if s < LAST:
+                read_out(s - 1, [SCALAR, SCALAR, SCALAR, VECTOR])
+
+        quantize_activity(LAST)
+        quantize_result(LAST - 2)
+        store_scales(y_scales_early, 0, early_columns)
+        read_out(LAST - 1, [SCALAR, SCALAR, VECTOR, VECTOR])
+        group_result(LAST - 1, GPSIMD)
+        read_out(LAST, [SCALAR, SCALAR, VECTOR, VECTOR])
+        turn_result(LAST - 1, [SCALAR, SCALAR, VECTOR])
+        turn_result(LAST, [SCALAR, VECTOR, SCALAR])
+        group_result(LAST, VECTOR)
+        quantize_result(LAST - 1)
+        quantize_result(LAST)
+        store_scales(y_scales_last, early_columns, B * C)

@@ -370,7 +370,8 @@ def tile_recurrent_rates_temporal_readout_h3_kernel(
             scale_activity(s, 1)
             turn_result(s - 2, [SCALAR] * C_TILES)
             if s < LAST:
-                read_out(s - 1, [SCALAR, SCALAR, SCALAR, VECTOR])
+                on_vector = 1 if pair + 1 < 2 * B else 2
+                read_out(s - 1, [SCALAR] * (PACK - on_vector) + [VECTOR] * on_vector)
 
         quantize_activity(LAST)
         quantize_result(LAST - 2)

from contextlib import ExitStack

import concourse.mybir as mybir
from concourse.masks import make_identity

B, T, N, C = 4, 512, 1024, 384
FLOPS = 2 * B * T * N * N + 2 * B * C * T * N

F32 = mybir.dt.float32
BF16 = mybir.dt.bfloat16
U32 = mybir.dt.uint32
I32 = mybir.dt.int32
U8 = mybir.dt.uint8
FP8X4 = mybir.dt.float8_e4m3fn_x4
FUNC = mybir.ActivationFunctionType
ALU = mybir.AluOpType
SCALAR, VECTOR, GPSIMD = "scalar", "vector", "gpsimd"

P = 128
PACK = 4
K_PASS = P * PACK
PASS_WORDS = K_PASS // 2
PASSES = N // K_PASS
C_TILES = C // P
CHUNK = 256
RUN = CHUNK // PACK
C_PARTS = ((0, 256), (256, C))
TURNING_BANKS = 7

UNITS = [(0, 0), (1, 0), (0, 1), (1, 1), (2, 0), (2, 1), (3, 0), (3, 1)]
LAST = len(UNITS) - 1


def tile_recurrent_rates_temporal_readout_h3_kernel(
    tc, rates, recurrent, time_gain, readout, offset, neuron_gain, out_0, out_1, out_2
):
    nc = tc.nc
    with ExitStack() as ctx:
        keep = ctx.enter_context(tc.tile_pool(name="keep", bufs=1))
        work2 = ctx.enter_context(tc.tile_pool(name="work2", bufs=2))
        work3 = ctx.enter_context(tc.tile_pool(name="work3", bufs=3))
        outp = ctx.enter_context(tc.tile_pool(name="outp", bufs=2 * C_TILES))
        psum = ctx.enter_context(tc.psum_pool(name="psum", bufs=1))
        ctx.enter_context(tc.manual_schedule())

        banks_taken = [0]

        def next_bank():
            k = banks_taken[0] % TURNING_BANKS
            banks_taken[0] = banks_taken[0] + 1
            return psum.tile([P, K_PASS], F32, name="bank%d" % k)

        def copy_on(engine, out, in_):
            if engine == SCALAR:
                nc.scalar.copy(out=out, in_=in_)
            else:
                nc.vector.tensor_copy(out=out, in_=in_)

        def interleave(engine, out, in_):
            if engine == GPSIMD:
                nc.gpsimd.tensor_scalar(
                    out=out, in0=in_.rearrange("p j c -> p c j"), scalar1=1.0, scalar2=0.0, op0=ALU.mult, op1=ALU.add
                )
            else:
                copy_on(engine, out.rearrange("p (c i) j -> p c j i", i=4), in_.rearrange("p j (c i) -> p c j i", i=4))

        def quantize(codes, scales, grouped):
            nc.vector.quantize_mx(out=codes.bitcast(FP8X4), scales=scales, in_=grouped)

        def quantize_components(codes, scales, grouped):
            flat = grouped.rearrange("p c j -> p (c j)")
            for c0, c1 in C_PARTS:
                quantize(codes[:, c0:c1], scales[:, c0:c1], flat[:, PACK * c0 : PACK * c1])

        rates_raw, weights_raw = {}, {}

        def load_rates(r, first=0, count=2):
            b, h = divmod(r, 2)
            raw = keep.tile([P, count, N], BF16, name="rates_raw%d_%d" % (r, first))
            t0 = 2 * h + first
            nc.sync.dma_start(out=raw[:], in_=rates[b].rearrange("(p t) k -> p t k", t=PACK)[:, t0 : t0 + count, :])
            for i in range(count):
                rates_raw[r, first + i] = raw[:, i, :]

        def load_weights(g, n0, width):
            weights_raw[g, n0] = keep.tile([P, PACK, width], BF16, name="weights_raw%d_%d" % (g, n0))
            rows = recurrent[g * K_PASS : (g + 1) * K_PASS, n0 : n0 + width]
            nc.sync.dma_start(out=weights_raw[g, n0][:], in_=rows.rearrange("(p j) n -> p j n", j=PACK))

        time_raw = keep.tile([P, PACK], BF16)
        offset_raw = keep.tile([P, PASSES, PACK], BF16)
        gain_raw = keep.tile([P, PASSES, PACK], BF16)
        readout_raw = keep.tile([P, C_TILES, T], BF16)

        nc.scalar.dma_start(out=time_raw[:], in_=time_gain.rearrange("(p t) -> p t", t=PACK))
        load_rates(0, 0, 1)
        load_rates(0, 1, 1)
        load_weights(0, 0, CHUNK)
        load_rates(1, 0, 1)
        load_weights(1, 0, CHUNK)
        load_rates(1, 1, 1)
        load_weights(0, CHUNK, CHUNK)
        load_weights(1, CHUNK, CHUNK)
        load_rates(2)
        load_weights(0, K_PASS, K_PASS)
        load_rates(3)
        load_weights(1, K_PASS, K_PASS)
        nc.sync.dma_start(out=readout_raw[:], in_=readout.rearrange("(i c) k -> c i k", c=P))
        nc.sync.dma_start(out=offset_raw[:], in_=offset.rearrange("(g p t) -> p g t", p=P, t=PACK))
        nc.sync.dma_start(out=gain_raw[:], in_=neuron_gain.rearrange("(g p t) -> p g t", p=P, t=PACK))
        for r in range(4, 2 * B):
            load_rates(r)

        ident = keep.tile([P, P], F32)
        make_identity(nc, ident[:])
        table_warm_up = keep.tile([P, 1], F32)
        nc.scalar.activation(out=table_warm_up[:], in_=ident[:, 0:1], func=FUNC.Tanh)

        rates_grouped, rates_codes, rates_scales = {}, {}, {}
        weights_grouped, weights_codes, weights_scales = {}, {}, {}
        tanh_drive, activity, activity_codes, activity_scales, y_neurons, y_grouped = {}, {}, {}, {}, {}, {}

        def turn_rates(r, engines):
            rates_grouped[r] = work3.tile([P, PASSES, 2, P, PACK], BF16, name="rates_grouped", align_bytes=64)
            words = rates_grouped[r][:].rearrange("p g t r j -> p g t (r j)").bitcast(F32)
            for t2 in range(2):
                src = rates_raw[r, t2].bitcast(F32)
                bank = next_bank()
                view = bank[:].rearrange("p (g u r) -> p g u r", g=PASSES, u=2)
                for g in range(PASSES):
                    for u in range(2):
                        every_second = src[:, PASS_WORDS * g + u : PASS_WORDS * (g + 1) : 2]
                        nc.tensor.transpose(view[:, g, u, :], every_second, ident[:])
                copy_on(
                    engines[t2],
                    words[:, :, t2, :].rearrange("p g (r u) -> p g r u", u=2),
                    view.rearrange("p g u r -> p g r u"),
                )

        def quantize_rates(r):
            rates_codes[r] = keep.tile([P, PASSES, 2, P], U32, name="rates_codes%d" % r, align_bytes=64)
            rates_scales[r] = keep.tile([P, PASSES, 2, P], U8, name="rates_scales%d" % r, align_bytes=64)
            quantize(
                rates_codes[r][:].rearrange("p g t r -> p (g t r)"),
                rates_scales[r][:].rearrange("p g t r -> p (g t r)"),
                rates_grouped[r][:].rearrange("p g t r j -> p (g t r j)"),
            )

        def group_weights(g, n0, engine):
            width = weights_raw[g, n0].shape[2]
            name = "shared_grouped" if width == K_PASS else "weights_grouped%d_%d" % (g, n0)
            weights_grouped[g, n0] = keep.tile([P, width, PACK], BF16, name=name, align_bytes=64)
            interleave(engine, weights_grouped[g, n0][:], weights_raw[g, n0][:])

        def quantize_weights(g, n0):
            width = weights_raw[g, n0].shape[2]
            codes = keep.tile([P, width], U32, name="weights_codes%d_%d" % (g, n0), align_bytes=64)
            scales = keep.tile([P, width], U8, name="weights_scales%d_%d" % (g, n0), align_bytes=64)
            quantize(codes[:], scales[:], weights_grouped[g, n0][:].rearrange("p n j -> p (n j)"))
            for c0 in range(0, width, CHUNK):
                weights_codes[g, n0 + c0] = codes[:, c0 : c0 + CHUNK]
                weights_scales[g, n0 + c0] = scales[:, c0 : c0 + CHUNK]

        readout_grouped = keep.tile([P, C, PACK], BF16, align_bytes=64)
        readout_codes = keep.tile([P, C], U32, align_bytes=64)
        readout_scales = keep.tile([P, C], U8, align_bytes=64)

        def turn_readout():
            words = readout_grouped[:].rearrange("p c j -> p (c j)").bitcast(F32)
            words = words.rearrange("p (i r u) -> p i r u", i=C_TILES, u=2)
            for first in range(0, C_TILES, 2):
                count = min(2, C_TILES - first)
                bank = next_bank()
                view = bank[:].rearrange("p (i u r) -> p i u r", i=2, u=2)
                for i in range(count):
                    src = readout_raw[:, first + i, :].bitcast(F32)
                    for u in range(2):
                        nc.tensor.transpose(view[:, i, u, :], src[:, u:PASS_WORDS:2], ident[:])
                nc.scalar.copy(out=words[:, first : first + count], in_=view[:, 0:count].rearrange("p i u r -> p i r u"))

        gain = keep.tile([P, PASSES, PACK], F32)
        shift = keep.tile([P, PASSES, PACK], F32)

        def prepare_gain_and_shift():
            nc.vector.tensor_copy(out=gain[:], in_=gain_raw[:])
            nc.vector.tensor_tensor(out=shift[:], in0=offset_raw[:], in1=gain_raw[:], op=ALU.mult)

        time_columns = keep.tile([P, P], F32)
        time_rows = keep.tile([P, P], F32)
        time_bank = psum.tile([P, K_PASS], F32, name="time_bank")

        def time_gain_to_rows():
            nc.gpsimd.memset(time_columns[:], 0.0)
            nc.gpsimd.tensor_copy(out=time_columns[:, 0:PACK], in_=time_raw[:])
            bank = next_bank()
            nc.tensor.transpose(bank[:, 0:P], time_columns[:], ident[:])
            nc.scalar.copy(out=time_rows[:], in_=bank[:, 0:P])

        def time_gain_to_psum():
            nc.tensor.transpose(time_bank[:, 0:P], time_rows[:], ident[:])

        def drive_bank(s, q, h):
            b, half = UNITS[s]
            if s not in tanh_drive:
                tanh_drive[s] = work2.tile([P, 2, 2, PACK, RUN, 2], F32, name="tanh_drive")
            bank = next_bank()
            view = bank[:].rearrange("p (t n) -> p t n", t=2)
            n0 = half * K_PASS + q * CHUNK
            for t2 in range(2):
                for g in range(PASSES):
                    nc.tensor.matmul_mx(
                        out=view[:, t2, :],
                        lhsT=rates_codes[2 * b + h][:, g, t2, :].bitcast(FP8X4),
                        lhsT_scale=rates_scales[2 * b + h][:, g, t2, :],
                        rhs=weights_codes[g, n0].bitcast(FP8X4),
                        rhs_scale=weights_scales[g, n0],
                        start=(g == 0),
                        stop=(g == PASSES - 1),
                    )
            nc.scalar.activation(
                out=tanh_drive[s][:, h, q], in_=view.rearrange("p t (m j) -> p j m t", j=PACK), func=FUNC.Tanh
            )

        def scale_activity(s, q):
            if s not in activity:
                activity[s] = work2.tile([P, K_PASS, PACK], BF16, name="activity", align_bytes=64)
            factor = time_bank[:, 0:PACK].rearrange("p (h t) -> p h t", t=2).unsqueeze(1).unsqueeze(1)
            nc.vector.tensor_tensor(
                out=activity[s][:].rearrange("p (j q m) (h t) -> p q j m h t", j=PACK, q=2, h=2)[:, q],
                in0=tanh_drive[s][:, :, q].rearrange("p h j m t -> p j m h t"),
                in1=factor.to_broadcast([P, PACK, RUN, 2, 2]),
                op=ALU.mult,
            )

        def quantize_activity(s):
            activity_codes[s] = work2.tile([P, K_PASS], U32, name="activity_codes", align_bytes=64)
            activity_scales[s] = work2.tile([P, K_PASS], U8, name="activity_scales", align_bytes=64)
            quantize(activity_codes[s][:], activity_scales[s][:], activity[s][:].rearrange("p n j -> p (n j)"))

        def read_out(s, engines):
            half = UNITS[s][1]
            y_neurons[s] = work3.tile([P, PACK, C], F32, name="y_neurons")
            for j in range(PACK):
                bank = next_bank()
                cols = slice(j * P, (j + 1) * P)
                for c0, c1 in C_PARTS:
                    nc.tensor.matmul_mx(
                        out=bank[:, c0:c1],
                        lhsT=activity_codes[s][:, cols].bitcast(FP8X4),
                        lhsT_scale=activity_scales[s][:, cols],
                        rhs=readout_codes[:, c0:c1].bitcast(FP8X4),
                        rhs_scale=readout_scales[:, c0:c1],
                        start=True,
                        stop=True,
                    )
                factor, addend = gain[:, half, j : j + 1], shift[:, half, j : j + 1]
                if engines[j] == SCALAR:
                    nc.scalar.activation(
                        out=y_neurons[s][:, j, :], in_=bank[:, 0:C], func=FUNC.Identity, scale=factor, bias=addend
                    )
                else:
                    nc.vector.tensor_scalar(
                        out=y_neurons[s][:, j, :],
                        in0=bank[:, 0:C],
                        scalar1=factor,
                        scalar2=addend,
                        op0=ALU.mult,
                        op1=ALU.add,
                    )

        def turn_result(s, engines):
            b, half = UNITS[s]
            for i in range(C_TILES):
                bank = next_bank()
                view = bank[:].rearrange("c (j p) -> c j p", j=PACK)
                for j in range(PACK):
                    nc.tensor.transpose(view[:, j, :], y_neurons[s][:, j, i * P : (i + 1) * P], ident[:])
                y = outp.tile([P, K_PASS], F32, name="y")
                copy_on(engines[i], y[:].rearrange("c (p j) -> c p j", j=PACK), view.rearrange("c j p -> c p j"))
                nc.sync.dma_start(out=out_0[b, i * P : (i + 1) * P, half * K_PASS : (half + 1) * K_PASS], in_=y[:])

        def group_result(s, engine):
            if engine == GPSIMD:
                y_grouped[s] = keep.tile([P, C, PACK], BF16, name="shared_grouped", align_bytes=64)
            else:
                y_grouped[s] = keep.tile([P, C, PACK], BF16, name="y_grouped", align_bytes=64)
            interleave(engine, y_grouped[s][:], y_neurons[s][:])

        early_columns = (B - 1) * C
        y_scales_early = keep.tile([P, PASSES, early_columns], U8, align_bytes=64)
        y_scales_last = keep.tile([P, PASSES, C], U8, align_bytes=64)

        def quantize_result(s):
            b, half = UNITS[s]
            y_codes = work3.tile([P, C], U32, name="y_codes", align_bytes=64)
            if b < B - 1:
                scales = y_scales_early[:, half, b * C : (b + 1) * C]
            else:
                scales = y_scales_last[:, half, :]
            quantize_components(y_codes[:], scales, y_grouped[s][:])
            nc.sync.dma_start(
                out=out_1[half, :, b * C : (b + 1) * C, :].rearrange("p m t -> p (m t)").bitcast(I32),
                in_=y_codes[:].bitcast(I32),
            )

        def store_scales(tile, m0, m1):
            for quadrant in range(4):
                nc.sync.dma_start(
                    out=out_2[:, 4 * quadrant : 4 * quadrant + 4, m0:m1].rearrange("g r m -> r g m").bitcast(I32),
                    in_=tile[32 * quadrant : 32 * quadrant + 4, :, :].bitcast(I32),
                )

        turn_rates(0, [VECTOR, SCALAR])
        time_gain_to_rows()
        group_weights(0, 0, VECTOR)
        turn_rates(1, [SCALAR, SCALAR])
        group_weights(1, 0, VECTOR)
        group_weights(0, CHUNK, SCALAR)
        time_gain_to_psum()
        quantize_rates(0)
        quantize_weights(0, 0)
        quantize_weights(1, 0)
        group_weights(1, CHUNK, VECTOR)
        drive_bank(0, 0, 0)
        quantize_rates(1)
        drive_bank(0, 0, 1)
        quantize_weights(0, CHUNK)
        quantize_weights(1, CHUNK)
        turn_rates(2, [SCALAR, SCALAR])
        group_weights(0, K_PASS, VECTOR)
        drive_bank(0, 1, 0)
        drive_bank(0, 1, 1)
        scale_activity(0, 0)
        quantize_rates(2)
        quantize_weights(0, K_PASS)
        turn_rates(3, [SCALAR, SCALAR])
        scale_activity(0, 1)
        quantize_rates(3)
        prepare_gain_and_shift()

        drive_bank(1, 0, 0)
        drive_bank(1, 1, 0)
        turn_readout()
        quantize_activity(0)
        quantize_components(readout_codes[:], readout_scales[:], readout_grouped[:])
        group_weights(1, K_PASS, VECTOR)
        drive_bank(1, 0, 1)
        drive_bank(1, 1, 1)
        quantize_weights(1, K_PASS)
        scale_activity(1, 0)
        scale_activity(1, 1)
        read_out(0, [SCALAR] * PACK)
        turn_rates(4, [SCALAR, SCALAR])

        for s in range(2, LAST + 1):
            pair = s + 2
            if 4 < pair < 2 * B:
                turn_rates(pair, [VECTOR, VECTOR])
            drive_bank(s, 0, 0)
            drive_bank(s, 0, 1)
            quantize_activity(s - 1)
            drive_bank(s, 1, 0)
            drive_bank(s, 1, 1)
            if pair < 2 * B:
                quantize_rates(pair)
            if s >= 3:
                quantize_result(s - 3)
            group_result(s - 2, GPSIMD)
            scale_activity(s, 0)
            scale_activity(s, 1)
            turn_result(s - 2, [SCALAR] * C_TILES)
            if s < LAST:
                on_vector = 1 if pair + 1 < 2 * B else 2
                read_out(s - 1, [SCALAR] * (PACK - on_vector) + [VECTOR] * on_vector)

        quantize_activity(LAST)
        quantize_result(LAST - 2)
        store_scales(y_scales_early, 0, early_columns)
        read_out(LAST - 1, [SCALAR, SCALAR, VECTOR, VECTOR])
        group_result(LAST - 1, GPSIMD)
        read_out(LAST, [SCALAR, SCALAR, VECTOR, VECTOR])
        turn_result(LAST - 1, [SCALAR, SCALAR, VECTOR])
        turn_result(LAST, [SCALAR, VECTOR, SCALAR])
        group_result(LAST, VECTOR)
        quantize_result(LAST - 1)
        quantize_result(LAST)
        store_scales(y_scales_last, early_columns, B * C)
